import numpy as np
import ml_dtypes


def mxq(x, axis, fmt="e4m3"):
    dtype, down = {"e4m3": (ml_dtypes.float8_e4m3fn, 7), "e5m2": (ml_dtypes.float8_e5m2, 14)}[fmt]
    v = np.moveaxis(np.asarray(x, np.float32).astype(ml_dtypes.bfloat16).astype(np.float64), axis, -1)
    blocks = v.reshape(v.shape[:-1] + (-1, 32))
    amax = np.abs(blocks).max(-1, keepdims=True)
    byte = np.maximum(np.where(amax > 0, np.frexp(amax)[1] - 1 + 127, 0) - down, 1)
    scale = np.exp2(byte - 127.0)
    codes = (blocks / scale).astype(np.float32).astype(dtype).astype(np.float64)
    return np.moveaxis((codes * scale).reshape(v.shape), -1, axis)


WIDE = False


def mx_kscale(k):
    if not WIDE:
        return np.ones(k)
    levels = np.array([10, -10, 5, -5, 0])
    if k % 512:
        return np.exp2(np.random.permutation(np.resize(levels, k // 32))).repeat(32)
    a = np.empty((k // 512, 16))
    for p in range(k // 512):
        a[p, :8] = np.random.permutation(np.resize(levels, 8))
        for g in range(8):
            far = levels[np.abs(levels - a[p, g]) >= 10]
            a[p, g + 8] = far[np.random.randint(len(far))]
    return np.exp2(a.ravel()).repeat(32)


def f64(x):
    return np.asarray(x).astype(np.float64)


def striped(idx):
    return np.tile(np.asarray(idx).reshape(-1, 16).T, (8, 1)).astype(np.uint16)


def unstriped(offs):
    return offs[:16].T.reshape(-1).astype(np.int64)


def striped8(idx):
    return np.asarray(idx).reshape(8, -1, 16).transpose(0, 2, 1).reshape(128, -1).astype(np.uint16)


def unstriped8(offs):
    return offs.reshape(8, 16, -1).transpose(0, 2, 1).reshape(8, -1).astype(np.int64)


def pick8(x, idx, run):
    r = np.arange(len(x))
    return x[r[:, None], idx[r % (8 * run) // run]]


E2M1 = np.array([0.0, 0.5, 1.0, 1.5, 2.0, 3.0, 4.0, 6.0, -0.0, -0.5, -1.0, -1.5, -2.0, -3.0, -4.0, -6.0])


def pack_weight(w, fmt):
    k, n = w.shape
    w = f64(np.asarray(w, np.float32).astype(ml_dtypes.bfloat16)).reshape(k // 32, 32, n)
    amax = np.abs(w).max(1)
    if fmt == "e4m3":
        byte = np.frexp(amax)[1] - 1 + 127 - 7
    else:
        mant, ex = np.frexp(amax / 6.0)
        byte = np.where(mant > 0.5, ex, ex - 1) + 127
    byte = np.clip(np.where(amax > 0, byte, 1), 1, 254)
    scaled = (w * np.exp2(127.0 - byte)[:, None, :]).reshape(k, n).astype(np.float32)
    by_word = np.ascontiguousarray(scaled.reshape(k // 512, 128, 4, n).transpose(0, 1, 3, 2))
    if fmt == "e4m3":
        words = by_word.astype(ml_dtypes.float8_e4m3fn).view(np.uint8)
    else:
        c = by_word.astype(ml_dtypes.float4_e2m1fn).view(np.uint8) & 0xF
        words = (c[..., 0::2] | (c[..., 1::2] << 4)).reshape(k // 512, 128, 2 * n)
    return np.ascontiguousarray(words), np.ascontiguousarray(byte.astype(np.uint8).reshape(k // 512, 16, n))


def unpack_weight(words, scales, fmt):
    g, _, n = scales.shape
    words = np.ascontiguousarray(words).reshape(g, 128, n, -1)
    if fmt == "e4m3":
        vals = words.view(ml_dtypes.float8_e4m3fn).astype(np.float64)
    else:
        nib = np.empty((g, 128, n, 4), np.uint8)
        nib[..., 0::2] = words & 0xF
        nib[..., 1::2] = words >> 4
        vals = E2M1[nib]
    vals = vals * np.repeat(np.exp2(scales.astype(np.float64) - 127.0), 8, axis=1)[..., None]
    return vals.transpose(0, 1, 3, 2).reshape(g * 512, n)


K, J, R, T, Z, M, C, O, N, S, U = 512, 256, 512, 1024, 512, 1024, 512, 256, 256, 1024, 512


def setup_inputs():
    n = np.random.standard_normal
    idx = np.random.permutation(T)[:J]
    idx2 = np.random.permutation(M)[:J]
    idx3 = np.stack([np.random.permutation(C)[:J] for _ in range(8)])
    idx4 = np.stack([np.random.permutation(C)[:J] for _ in range(8)])
    idx5 = np.random.permutation(S)[:N]
    idx6 = np.stack([np.random.permutation(U)[:O] for _ in range(8)])
    idx7 = np.stack([np.random.permutation(U)[:O] for _ in range(8)])
    fk = mx_kscale(K)
    fr = mx_kscale(R)
    fz = mx_kscale(Z)
    xtp = pack_weight(n((K, T)) * fk[:, None], "e2m1")
    wp = pack_weight(n((K, R)) * 1 / np.sqrt(K) / fk[:, None] * fr, "e4m3")
    xop = pack_weight(n((Z, M)) / fz[:, None], "e4m3")
    w2p = pack_weight(n((Z, R)) * 1 / np.sqrt(Z) * fz[:, None] * fr, "e2m1")
    vsp = pack_weight(n((R, S)) * 1 / np.sqrt(R) / fr[:, None], "e2m1")
    return {
        "xt_words": xtp[0],
        "xt_scales": xtp[1],
        "w_words": wp[0],
        "w_scales": wp[1],
        "xo_words": xop[0],
        "xo_scales": xop[1],
        "w2_words": w2p[0],
        "w2_scales": w2p[1],
        "vs_words": vsp[0],
        "vs_scales": vsp[1],
        "offs": striped(idx),
        "offs2": striped(idx2),
        "offs3": striped8(idx3),
        "offs4": striped8(idx4),
        "offs5": striped(idx5),
        "offs6": striped8(idx6),
        "offs7": striped8(idx7),
    }


def reference(xt_words, xt_scales, w_words, w_scales, xo_words, xo_scales, w2_words, w2_scales, vs_words, vs_scales, offs, offs2, offs3, offs4, offs5, offs6, offs7):
    idx = unstriped(offs)
    idx2 = unstriped(offs2)
    idx3 = unstriped8(offs3)
    idx4 = unstriped8(offs4)
    idx5 = unstriped(offs5)
    idx6 = unstriped8(offs6)
    idx7 = unstriped8(offs7)
    xtu = unpack_weight(xt_words, xt_scales, "e2m1")
    wu = unpack_weight(w_words, w_scales, "e4m3")
    xou = unpack_weight(xo_words, xo_scales, "e4m3")
    w2u = unpack_weight(w2_words, w2_scales, "e2m1")
    vsu = unpack_weight(vs_words, vs_scales, "e2m1")
    xtidxg = xtu[:, idx]
    a = wu.T @ xtidxg
    xoidx2g = xou[:, idx2]
    b = w2u.T @ xoidx2g
    pw = np.zeros((R, C))
    pw[np.arange(R)[:, None], idx3[np.arange(R) % 512 // 64]] = a
    pv = np.zeros((R, C))
    pv[np.arange(R)[:, None], idx4[np.arange(R) % 512 // 64]] = b
    pg = pw + pv
    hid = pg.reshape(R, O, C // O).max(axis=2)
    vsidx5g = vsu[:, idx5]
    hidq = mxq(hid, 0, "e4m3")
    p = vsidx5g.T @ hidq
    m0 = np.zeros((N, U))
    m0[np.arange(N)[:, None], idx6[np.arange(N) % 128 // 16]] = p
    m1 = np.zeros((N, U))
    m1[np.arange(N)[:, None], idx7[np.arange(N) % 128 // 16]] = p
    y = m0 - m1
    return y

@@ -1,0 +1,295 @@
+from contextlib import ExitStack
+
+import concourse.mybir as mybir
+
+F32 = mybir.dt.float32
+BF16 = mybir.dt.bfloat16
+I32 = mybir.dt.int32
+U32 = mybir.dt.uint32
+U16 = mybir.dt.uint16
+U8 = mybir.dt.uint8
+FP8X4 = mybir.dt.float8_e4m3fn_x4
+FP4X4 = mybir.dt.float4_e2m1fn_x4
+COPY = mybir.ActivationFunctionType.Copy
+ALU = mybir.AluOpType
+
+P = 128
+PACK = 4
+J = 256
+R = 512
+STORE = 1024
+BOARD = 512
+POOLS = 256
+PAGE = 512
+HALF = 128
+QUARTER = 64
+FLOPS = 2 * 512 * 512 * 256 * 2 + 2 * 512 * 256 * 256
+
+
+def tile_picked_tokens_plain_two_pooledboard_store_divergence_kernel(
+    tc, xt_words, xt_scales, w_words, w_scales, xo_words, xo_scales, w2_words, w2_scales,
+    vs_words, vs_scales, offs, offs2, offs3, offs4, offs5, offs6, offs7, out,
+):
+    nc = tc.nc
+
+    with ExitStack() as ctx:
+        lists = ctx.enter_context(tc.tile_pool(name="lists", bufs=1))
+        sb = ctx.enter_context(tc.tile_pool(name="sb", bufs=1))
+        psum = ctx.enter_context(tc.psum_pool(name="psum", bufs=1))
+
+        def tile(shape, dtype, name, tag=None):
+            return sb.tile(shape, dtype, name=name, tag=tag or name, align_bytes=64)
+
+        def load_list(source, name):
+            held = lists.tile([P, J // 16], U16, name=name)
+            nc.sync.dma_start(held[:], source)
+            return held
+
+        def entries(held, start, count):
+            return held[:, start // 16 : (start + count) // 16]
+
+        def zero(engine, target):
+            engine.memset(target, 0)
+
+        def load_scales(plane, scales):
+            for q in range(4):
+                nc.sync.dma_start(
+                    plane[32 * q : 32 * q + 4, :].bitcast(I32),
+                    scales[0, 4 * q : 4 * q + 4, :].bitcast(I32),
+                )
+
+        def load_folded_scales(folded, scales):
+            rows = scales[0].rearrange("(h g i) n -> g i h n", h=2, g=2, i=4)
+            for g in range(2):
+                nc.sync.dma_start(
+                    folded[32 * g : 32 * g + 4, :, :].bitcast(I32), rows[g].bitcast(I32)
+                )
+
+        def unfold_and_deal_scales(dealt, folded):
+            nc.vector.tensor_copy(
+                folded[64:128, 0, :].bitcast(I32), folded[0:64, 1, :].bitcast(I32)
+            )
+            nc.vector.tensor_copy(
+                dealt[:], folded[:, 0, :].rearrange("p (m t) -> p t m", t=PACK)
+            )
+
+        def scatter(window, held, start, count, values):
+            nc.scalar.activation(window[:].indirect(entries(held, start, count)), values, COPY)
+
+        w_folded = tile([P, 2, R], U8, "w_folded")
+        xt_plane = tile([P, STORE], U8, "xt_plane")
+        zero(nc.vector, w_folded[:].rearrange("p h n -> p (h n)").bitcast(I32))
+        zero(nc.vector, xt_plane[:].bitcast(I32))
+
+        xt_raw = tile([P, STORE], U16, "xt_raw")
+        w_raw = tile([P, R], U32, "w_raw")
+        nc.scalar.dma_start(xt_raw[:].bitcast(I32), xt_words[0].bitcast(I32))
+        nc.scalar.dma_start(
+            w_raw[:].bitcast(I32), w_words[0].rearrange("p n t -> p (n t)").bitcast(I32)
+        )
+        idx = load_list(offs, "idx")
+        load_folded_scales(w_folded, w_scales)
+        load_scales(xt_plane, xt_scales)
+        idx3 = load_list(offs3, "idx3")
+
+        pw = [tile([P, BOARD], F32, "pw%d" % t) for t in range(PACK)]
+        w2_folded = tile([P, 2, R], U8, "w2_folded")
+        xo_plane = tile([P, STORE], U8, "xo_plane")
+        vs_plane = tile([P, STORE], U8, "vs_plane")
+        zero(nc.vector, pw[0][:])
+        zero(nc.vector, w2_folded[:].rearrange("p h n -> p (h n)").bitcast(I32))
+        zero(nc.vector, xo_plane[:].bitcast(I32))
+        zero(nc.vector, vs_plane[:].bitcast(I32))
+
+        xo_raw = tile([P, STORE], U32, "xo_raw")
+        w2_raw = tile([P, 2 * R], U8, "w2_raw")
+        vs_raw = tile([P, STORE], U16, "vs_raw")
+        nc.sync.dma_start(
+            xo_raw[:].bitcast(I32), xo_words[0].rearrange("p n t -> p (n t)").bitcast(I32)
+        )
+        nc.sync.dma_start(w2_raw[:].bitcast(I32), w2_words[0].bitcast(I32))
+        idx2 = load_list(offs2, "idx2")
+        load_folded_scales(w2_folded, w2_scales)
+        load_scales(xo_plane, xo_scales)
+        idx4 = load_list(offs4, "idx4")
+        nc.sync.dma_start(vs_raw[:].bitcast(I32), vs_words[0].bitcast(I32))
+        idx5 = load_list(offs5, "idx5")
+        load_scales(vs_plane, vs_scales)
+        idx6 = load_list(offs6, "idx6")
+        idx7 = load_list(offs7, "idx7")
+
+        w_codes = tile([P, PACK, P], U32, "w_codes")
+        w_plane = tile([P, PACK, P], U8, "w_plane")
+        xt_codes = tile([P, 2 * J], U8, "xt_codes")
+        xt_bytes = tile([P, J], U8, "xt_bytes")
+        a_sb = tile([P, 2, PACK, HALF], F32, "a_sb")
+        a_first = psum.tile([P, HALF], F32, name="a_first")
+        a_next = psum.tile([P, PACK - 1, HALF], F32, name="a_next")
+        a_late = psum.tile([P, PACK, HALF], F32, name="a_late")
+
+        def gather_xt(h):
+            nc.vector.tensor_copy(
+                xt_codes[:, 2 * HALF * h : 2 * HALF * (h + 1)].bitcast(U16),
+                xt_raw[:].indirect(entries(idx, HALF * h, HALF)),
+            )
+            nc.vector.tensor_copy(
+                xt_bytes[:, HALF * h : HALF * (h + 1)],
+                xt_plane[:].indirect(entries(idx, HALF * h, HALF)),
+            )
+
+        def multiply_a(target, t, h):
+            nc.tensor.matmul_mx(
+                out=target,
+                lhsT=w_codes[:, t, :].bitcast(FP8X4),
+                lhsT_scale=w_plane[:, t, :],
+                rhs=xt_codes[:, 2 * HALF * h : 2 * HALF * (h + 1)].bitcast(FP4X4),
+                rhs_scale=xt_bytes[:, HALF * h : HALF * (h + 1)],
+                start=True,
+                stop=True,
+            )
+
+        w_by_row = w_raw[:].rearrange("p (m t) -> p m t", t=PACK)
+        unfold_and_deal_scales(w_plane, w_folded)
+        nc.vector.tensor_copy(w_codes[:, 0, :], w_by_row[:, :, 0])
+        gather_xt(0)
+        multiply_a(a_first[:], 0, 0)
+        nc.scalar.activation(a_sb[:, 0, 0, :], a_first[:], COPY)
+        scatter(pw[0], idx3, 0, HALF, a_sb[:, 0, 0, :])
+
+        nc.vector.tensor_copy(
+            w_codes[:, 1:PACK, :].rearrange("p t m -> p m t"), w_by_row[:, :, 1:PACK]
+        )
+        for t in range(1, PACK):
+            multiply_a(a_next[:, t - 1, :], t, 0)
+            zero(nc.vector, pw[t][:])
+        nc.vector.tensor_copy(a_sb[:, 0, 1:PACK, :], a_next[:])
+        for t in range(1, PACK):
+            scatter(pw[t], idx3, 0, HALF, a_sb[:, 0, t, :])
+
+        gather_xt(1)
+        for t in range(PACK):
+            multiply_a(a_late[:, t, :], t, 1)
+        nc.vector.tensor_copy(a_sb[:, 1, :, :], a_late[:])
+        for t in range(PACK):
+            scatter(pw[t], idx3, HALF, HALF, a_sb[:, 1, t, :])
+
+        w2_codes = tile([P, PACK, P, 2], U8, "w2_codes")
+        w2_plane = tile([P, PACK, P], U8, "w2_plane")
+        xo_codes = tile([P, J], U32, "xo_codes")
+        xo_bytes = tile([P, J], U8, "xo_bytes")
+        b_sb = tile([P, PACK, J], F32, "b_sb")
+        unfold_and_deal_scales(w2_plane, w2_folded)
+        nc.vector.tensor_copy(
+            w2_codes[:], w2_raw[:].rearrange("p (m t e) -> p t m e", t=PACK, e=2)
+        )
+        nc.vector.tensor_copy(xo_codes[:], xo_raw[:].indirect(idx2[:]))
+        nc.vector.tensor_copy(xo_bytes[:], xo_plane[:].indirect(idx2[:]))
+        pv = [tile([P, BOARD], F32, "pv0", tag="xt_raw"), tile([P, BOARD], F32, "pv1", tag="w_raw")]
+        for window in pv:
+            zero(nc.vector, window[:])
+        for pair in range(2):
+            bank = psum.tile([P, 2, J], F32, name="b_bank%d" % pair)
+            for u in range(2):
+                t = 2 * pair + u
+                nc.tensor.matmul_mx(
+                    out=bank[:, u, :],
+                    lhsT=w2_codes[:, t, :, :].rearrange("p m e -> p (m e)").bitcast(FP4X4),
+                    lhsT_scale=w2_plane[:, t, :],
+                    rhs=xo_codes[:].bitcast(FP8X4),
+                    rhs_scale=xo_bytes[:],
+                    start=True,
+                    stop=True,
+                )
+            nc.vector.tensor_copy(b_sb[:, 2 * pair : 2 * pair + 2, :], bank[:])
+
+        vs_codes = tile([P, 2 * J], U8, "vs_codes")
+        vs_bytes = tile([P, J], U8, "vs_bytes")
+        nc.vector.tensor_copy(vs_codes[:].bitcast(U16), vs_raw[:].indirect(idx5[:]))
+        nc.vector.tensor_copy(vs_bytes[:], vs_plane[:].indirect(idx5[:]))
+
+        hid = tile([P, POOLS, PACK], BF16, "hid")
+        pg = tile([P, POOLS, 2], F32, "pg", tag="vs_raw")
+        pg_flat = pg[:].rearrange("p o e -> p (o e)")
+
+        def add_boards(t, o0, count):
+            cols = slice(2 * o0, 2 * (o0 + count))
+            nc.vector.tensor_tensor(pg_flat[:, cols], pw[t][:, cols], pv[t % 2][:, cols], ALU.add)
+
+        def pool_board(t, o0, count):
+            pools = slice(o0, o0 + count)
+            nc.vector.tensor_tensor(hid[:, pools, t], pg[:, pools, 0], pg[:, pools, 1], ALU.max)
+
+        hid_codes = tile([P, POOLS], U32, "hid_codes")
+        hid_bytes = tile([P, POOLS], U8, "hid_bytes")
+
+        def quantise(o0, count):
+            pools = slice(o0, o0 + count)
+            nc.vector.quantize_mx(
+                out=hid_codes[:, pools].bitcast(FP8X4),
+                scales=hid_bytes[:, pools],
+                in_=hid[:, pools, :].rearrange("p o t -> p (o t)"),
+            )
+
+        m0 = []
+        m1 = []
+        for t in range(PACK - 1):
+            scatter(pv[t % 2], idx4, 0, J, b_sb[:, t, :])
+            add_boards(t, 0, POOLS)
+            pool_board(t, 0, POOLS)
+        m0.append(tile([P, PAGE], F32, "m0_0", tag="xo_raw"))
+        m1.append(tile([P, PAGE], F32, "m1_0", tag="w2_raw"))
+        m0.append(tile([P, PAGE], F32, "m0_1", tag="pw0"))
+        m1.append(tile([P, PAGE], F32, "m1_1", tag="pw1"))
+        for window in m0 + m1:
+            zero(nc.gpsimd, window[:])
+
+        last = PACK - 1
+        scatter(pv[last % 2], idx4, 0, J, b_sb[:, last, :])
+        p_sb = tile([P, 2, POOLS], F32, "p_sb")
+        p_first = psum.tile([P, HALF], F32, name="p_first")
+        p_next = psum.tile([P, HALF], F32, name="p_next")
+        p_late = psum.tile([P, 2, HALF], F32, name="p_late")
+
+        def multiply_p(target, u, h):
+            pools = slice(HALF * h, HALF * (h + 1))
+            nc.tensor.matmul_mx(
+                out=target,
+                lhsT=vs_codes[:, 2 * P * u : 2 * P * (u + 1)].bitcast(FP4X4),
+                lhsT_scale=vs_bytes[:, P * u : P * (u + 1)],
+                rhs=hid_codes[:, pools].bitcast(FP8X4),
+                rhs_scale=hid_bytes[:, pools],
+                start=True,
+                stop=True,
+            )
+
+        quarters = (0, QUARTER)
+        for step in (add_boards, pool_board):
+            for o0 in quarters:
+                step(last, o0, QUARTER)
+        for o0 in quarters:
+            quantise(o0, QUARTER)
+        multiply_p(p_first[:], 0, 0)
+        multiply_p(p_next[:], 1, 0)
+        nc.scalar.activation(p_sb[:, 0, 0:HALF], p_first[:], COPY)
+        scatter(m0[0], idx6, 0, HALF, p_sb[:, 0, 0:HALF])
+        scatter(m1[0], idx7, 0, HALF, p_sb[:, 0, 0:HALF])
+
+        add_boards(last, HALF, HALF)
+        pool_board(last, HALF, HALF)
+        quantise(HALF, HALF)
+        for u in (0, 1):
+            multiply_p(p_late[:, u, :], u, 1)
+        nc.vector.tensor_copy(p_sb[:, :, HALF:POOLS], p_late[:])
+        nc.vector.tensor_copy(p_sb[:, 1, 0:HALF], p_next[:])
+        scatter(m0[0], idx6, HALF, HALF, p_sb[:, 0, HALF:POOLS])
+        scatter(m1[0], idx7, HALF, HALF, p_sb[:, 0, HALF:POOLS])
+        scatter(m0[1], idx6, 0, J, p_sb[:, 1, :])
+        scatter(m1[1], idx7, 0, J, p_sb[:, 1, :])
+
+        y = tile([P, 2, PAGE], F32, "y")
+        nc.vector.tensor_tensor(y[:, 0, :], m0[0][:], m1[0][:], ALU.subtract)
+        nc.sync.dma_start(out[0:P, :], y[:, 0, :])
+        for h, queue in enumerate((nc.sync, nc.scalar)):
+            cols = slice(h * PAGE // 2, (h + 1) * PAGE // 2)
+            nc.vector.tensor_tensor(y[:, 1, cols], m0[1][:, cols], m1[1][:, cols], ALU.subtract)
+            queue.dma_start(out[P : 2 * P, cols], y[:, 1, cols])

@@ -23,6 +23,7 @@ POOLS = 256
 PAGE = 512
 HALF = 128
 QUARTER = 64
+RUN = 4
 FLOPS = 2 * 512 * 512 * 256 * 2 + 2 * 512 * 256 * 256
 
 
@@ -49,7 +50,7 @@ def tile_picked_tokens_plain_two_pooledboard_store_divergence_kernel(
             return held[:, start // 16 : (start + count) // 16]
 
         def zero(engine, target):
-            engine.memset(target, 0)
+            engine.memset(target.bitcast(I32), 0)
 
         def load_scales(plane, scales):
             for q in range(4):
@@ -58,48 +59,42 @@ def tile_picked_tokens_plain_two_pooledboard_store_divergence_kernel(
                     scales[0, 4 * q : 4 * q + 4, :].bitcast(I32),
                 )
 
-        def load_folded_scales(folded, scales):
-            rows = scales[0].rearrange("(h g i) n -> g i h n", h=2, g=2, i=4)
-            for g in range(2):
-                nc.sync.dma_start(
-                    folded[32 * g : 32 * g + 4, :, :].bitcast(I32), rows[g].bitcast(I32)
-                )
-
-        def unfold_and_deal_scales(dealt, folded):
-            nc.vector.tensor_copy(
-                folded[64:128, 0, :].bitcast(I32), folded[0:64, 1, :].bitcast(I32)
-            )
-            nc.vector.tensor_copy(
-                dealt[:], folded[:, 0, :].rearrange("p (m t) -> p t m", t=PACK)
-            )
+        def deal_scales(engine, dealt, plane):
+            engine.tensor_copy(dealt[:], plane[:].rearrange("p (m t) -> p t m", t=PACK))
 
         def scatter(window, held, start, count, values):
             nc.scalar.activation(window[:].indirect(entries(held, start, count)), values, COPY)
 
-        w_folded = tile([P, 2, R], U8, "w_folded")
         xt_plane = tile([P, STORE], U8, "xt_plane")
-        zero(nc.vector, w_folded[:].rearrange("p h n -> p (h n)").bitcast(I32))
-        zero(nc.vector, xt_plane[:].bitcast(I32))
+        w_spread = tile([P, R], U8, "w_spread")
+        zero(nc.vector, xt_plane[:])
+        zero(nc.vector, w_spread[:])
 
+        w_staged = tile([4, 4, R], U8, "w_staged")
         xt_raw = tile([P, STORE], U16, "xt_raw")
         w_raw = tile([P, R], U32, "w_raw")
-        nc.scalar.dma_start(xt_raw[:].bitcast(I32), xt_words[0].bitcast(I32))
-        nc.scalar.dma_start(
+        nc.sync.dma_start(
+            w_staged[:].bitcast(I32),
+            w_scales[0].rearrange("(q i) n -> i q n", i=4).bitcast(I32),
+        )
+        nc.sync.dma_start(xt_raw[:].bitcast(I32), xt_words[0].bitcast(I32))
+        nc.sync.dma_start(
             w_raw[:].bitcast(I32), w_words[0].rearrange("p n t -> p (n t)").bitcast(I32)
         )
         idx = load_list(offs, "idx")
-        load_folded_scales(w_folded, w_scales)
         load_scales(xt_plane, xt_scales)
         idx3 = load_list(offs3, "idx3")
 
         pw = [tile([P, BOARD], F32, "pw%d" % t) for t in range(PACK)]
-        w2_folded = tile([P, 2, R], U8, "w2_folded")
+        w2_spread = tile([P, R], U8, "w2_spread")
         xo_plane = tile([P, STORE], U8, "xo_plane")
+        for t in range(PACK - 1):
+            zero(nc.vector, pw[t][:])
+        zero(nc.gpsimd, xo_plane[:])
+        zero(nc.gpsimd, w2_spread[:])
+        zero(nc.gpsimd, pw[PACK - 1][:])
         vs_plane = tile([P, STORE], U8, "vs_plane")
-        zero(nc.vector, pw[0][:])
-        zero(nc.vector, w2_folded[:].rearrange("p h n -> p (h n)").bitcast(I32))
-        zero(nc.vector, xo_plane[:].bitcast(I32))
-        zero(nc.vector, vs_plane[:].bitcast(I32))
+        zero(nc.gpsimd, vs_plane[:])
 
         xo_raw = tile([P, STORE], U32, "xo_raw")
         w2_raw = tile([P, 2 * R], U8, "w2_raw")
@@ -109,8 +104,8 @@ def tile_picked_tokens_plain_two_pooledboard_store_divergence_kernel(
         )
         nc.sync.dma_start(w2_raw[:].bitcast(I32), w2_words[0].bitcast(I32))
         idx2 = load_list(offs2, "idx2")
-        load_folded_scales(w2_folded, w2_scales)
         load_scales(xo_plane, xo_scales)
+        load_scales(w2_spread, w2_scales)
         idx4 = load_list(offs4, "idx4")
         nc.sync.dma_start(vs_raw[:].bitcast(I32), vs_words[0].bitcast(I32))
         idx5 = load_list(offs5, "idx5")
@@ -120,71 +115,71 @@ def tile_picked_tokens_plain_two_pooledboard_store_divergence_kernel(
 
         w_codes = tile([P, PACK, P], U32, "w_codes")
         w_plane = tile([P, PACK, P], U8, "w_plane")
-        xt_codes = tile([P, 2 * J], U8, "xt_codes")
-        xt_bytes = tile([P, J], U8, "xt_bytes")
-        a_sb = tile([P, 2, PACK, HALF], F32, "a_sb")
-        a_first = psum.tile([P, HALF], F32, name="a_first")
-        a_next = psum.tile([P, PACK - 1, HALF], F32, name="a_next")
-        a_late = psum.tile([P, PACK, HALF], F32, name="a_late")
 
         def gather_xt(h):
-            nc.vector.tensor_copy(
-                xt_codes[:, 2 * HALF * h : 2 * HALF * (h + 1)].bitcast(U16),
-                xt_raw[:].indirect(entries(idx, HALF * h, HALF)),
-            )
-            nc.vector.tensor_copy(
-                xt_bytes[:, HALF * h : HALF * (h + 1)],
-                xt_plane[:].indirect(entries(idx, HALF * h, HALF)),
-            )
+            codes = tile([P, 2 * HALF], U8, "xt_codes%d" % h, tag="xt_codes")
+            scale_bytes = tile([P, HALF], U8, "xt_bytes%d" % h, tag="xt_bytes")
+            listed = entries(idx, HALF * h, HALF)
+            nc.vector.tensor_copy(codes[:].bitcast(U16), xt_raw[:].indirect(listed))
+            nc.vector.tensor_copy(scale_bytes[:], xt_plane[:].indirect(listed))
+            return codes, scale_bytes
 
-        def multiply_a(target, t, h):
+        def multiply_a(target, t, gathered):
+            codes, scale_bytes = gathered
             nc.tensor.matmul_mx(
                 out=target,
                 lhsT=w_codes[:, t, :].bitcast(FP8X4),
                 lhsT_scale=w_plane[:, t, :],
-                rhs=xt_codes[:, 2 * HALF * h : 2 * HALF * (h + 1)].bitcast(FP4X4),
-                rhs_scale=xt_bytes[:, HALF * h : HALF * (h + 1)],
+                rhs=codes[:].bitcast(FP4X4),
+                rhs_scale=scale_bytes[:],
                 start=True,
                 stop=True,
             )
 
         w_by_row = w_raw[:].rearrange("p (m t) -> p m t", t=PACK)
-        unfold_and_deal_scales(w_plane, w_folded)
+        for q in range(4):
+            nc.vector.tensor_copy(
+                w_spread[32 * q : 32 * q + 4, :].bitcast(I32), w_staged[:, q, :].bitcast(I32)
+            )
+        deal_scales(nc.vector, w_plane, w_spread)
         nc.vector.tensor_copy(w_codes[:, 0, :], w_by_row[:, :, 0])
-        gather_xt(0)
-        multiply_a(a_first[:], 0, 0)
-        nc.scalar.activation(a_sb[:, 0, 0, :], a_first[:], COPY)
-        scatter(pw[0], idx3, 0, HALF, a_sb[:, 0, 0, :])
-
+        gathered = gather_xt(0)
+        first = psum.tile([P, 1, HALF], F32, name="a_first", tag="bank0")
+        multiply_a(first[:, 0, :], 0, gathered)
+        a_first = tile([P, HALF], F32, "a_first_sb")
+        nc.scalar.activation(a_first[:], first[:, 0, :], COPY)
+        scatter(pw[0], idx3, 0, HALF, a_first[:])
         nc.vector.tensor_copy(
             w_codes[:, 1:PACK, :].rearrange("p t m -> p m t"), w_by_row[:, :, 1:PACK]
         )
-        for t in range(1, PACK):
-            multiply_a(a_next[:, t - 1, :], t, 0)
-            zero(nc.vector, pw[t][:])
-        nc.vector.tensor_copy(a_sb[:, 0, 1:PACK, :], a_next[:])
-        for t in range(1, PACK):
-            scatter(pw[t], idx3, 0, HALF, a_sb[:, 0, t, :])
 
-        gather_xt(1)
-        for t in range(PACK):
-            multiply_a(a_late[:, t, :], t, 1)
-        nc.vector.tensor_copy(a_sb[:, 1, :, :], a_late[:])
-        for t in range(PACK):
-            scatter(pw[t], idx3, HALF, HALF, a_sb[:, 1, t, :])
+        def put_a(h, tiles, gathered, tag):
+            bank = psum.tile([P, len(tiles), HALF], F32, name="a_%d_%d" % (h, tiles[0]), tag=tag)
+            for u, t in enumerate(tiles):
+                multiply_a(bank[:, u, :], t, gathered)
+            values = tile([P, len(tiles), HALF], F32, "a_sb_%d_%d" % (h, tiles[0]))
+            nc.vector.tensor_copy(values[:], bank[:])
+            for u, t in enumerate(tiles):
+                scatter(pw[t], idx3, HALF * h, HALF, values[:, u, :])
 
-        w2_codes = tile([P, PACK, P, 2], U8, "w2_codes")
-        w2_plane = tile([P, PACK, P], U8, "w2_plane")
-        xo_codes = tile([P, J], U32, "xo_codes")
-        xo_bytes = tile([P, J], U8, "xo_bytes")
-        b_sb = tile([P, PACK, J], F32, "b_sb")
-        unfold_and_deal_scales(w2_plane, w2_folded)
-        nc.vector.tensor_copy(
+        put_a(0, [1], gathered, "bank1")
+        put_a(0, [2, 3], gathered, "bank2")
+        gathered = gather_xt(1)
+        put_a(1, [0, 1], gathered, "bank3")
+        put_a(1, [2, 3], gathered, "bank4")
+
+        w2_codes = tile([P, PACK, P, 2], U8, "w2_codes", tag="w_codes")
+        w2_plane = tile([P, PACK, P], U8, "w2_plane", tag="w_plane")
+        xo_codes = tile([P, J], U32, "xo_codes", tag="xt_codes")
+        xo_bytes = tile([P, J], U8, "xo_bytes", tag="xt_bytes")
+        b_sb = [tile([P, 2, J], F32, "b_sb%d" % pair) for pair in range(2)]
+        nc.gpsimd.tensor_copy(
             w2_codes[:], w2_raw[:].rearrange("p (m t e) -> p t m e", t=PACK, e=2)
         )
+        deal_scales(nc.gpsimd, w2_plane, w2_spread)
         nc.vector.tensor_copy(xo_codes[:], xo_raw[:].indirect(idx2[:]))
         nc.vector.tensor_copy(xo_bytes[:], xo_plane[:].indirect(idx2[:]))
-        pv = [tile([P, BOARD], F32, "pv0", tag="xt_raw"), tile([P, BOARD], F32, "pv1", tag="w_raw")]
+        pv = [tile([P, BOARD], F32, "pv0", tag="xo_raw"), tile([P, BOARD], F32, "pv1", tag="xo_plane")]
         for window in pv:
             zero(nc.vector, window[:])
         for pair in range(2):
@@ -200,55 +195,60 @@ def tile_picked_tokens_plain_two_pooledboard_store_divergence_kernel(
                     start=True,
                     stop=True,
                 )
-            nc.vector.tensor_copy(b_sb[:, 2 * pair : 2 * pair + 2, :], bank[:])
+            nc.vector.tensor_copy(b_sb[pair][:], bank[:])
 
-        vs_codes = tile([P, 2 * J], U8, "vs_codes")
-        vs_bytes = tile([P, J], U8, "vs_bytes")
+        vs_codes = tile([P, 2 * J], U8, "vs_codes", tag="w_codes")
+        vs_bytes = tile([P, J], U8, "vs_bytes", tag="w_plane")
         nc.vector.tensor_copy(vs_codes[:].bitcast(U16), vs_raw[:].indirect(idx5[:]))
         nc.vector.tensor_copy(vs_bytes[:], vs_plane[:].indirect(idx5[:]))
 
-        hid = tile([P, POOLS, PACK], BF16, "hid")
-        pg = tile([P, POOLS, 2], F32, "pg", tag="vs_raw")
-        pg_flat = pg[:].rearrange("p o e -> p (o e)")
+        pg = tile([P, PACK, BOARD], F32, "pg", tag="vs_raw")
 
         def add_boards(t, o0, count):
             cols = slice(2 * o0, 2 * (o0 + count))
-            nc.vector.tensor_tensor(pg_flat[:, cols], pw[t][:, cols], pv[t % 2][:, cols], ALU.add)
+            nc.vector.tensor_tensor(pg[:, t, cols], pw[t][:, cols], pv[t % 2][:, cols], ALU.add)
 
-        def pool_board(t, o0, count):
-            pools = slice(o0, o0 + count)
-            nc.vector.tensor_tensor(hid[:, pools, t], pg[:, pools, 0], pg[:, pools, 1], ALU.max)
+        def pool_boards(hid, h0, o0, count):
+            pairs = pg[:, :, 2 * o0 : 2 * (o0 + count)].rearrange(
+                "p t (c i e) -> p c t i e", i=RUN, e=2
+            )
+            nc.vector.tensor_tensor(
+                hid[:, h0 : h0 + count, :].rearrange("p (c i) t -> p c t i", i=RUN),
+                pairs[:, :, :, :, 0],
+                pairs[:, :, :, :, 1],
+                ALU.max,
+            )
 
         hid_codes = tile([P, POOLS], U32, "hid_codes")
         hid_bytes = tile([P, POOLS], U8, "hid_bytes")
 
-        def quantise(o0, count):
+        def quantise(hid, h0, o0, count):
             pools = slice(o0, o0 + count)
             nc.vector.quantize_mx(
                 out=hid_codes[:, pools].bitcast(FP8X4),
                 scales=hid_bytes[:, pools],
-                in_=hid[:, pools, :].rearrange("p o t -> p (o t)"),
+                in_=hid[:, h0 : h0 + count, :].rearrange("p o t -> p (o t)"),
             )
 
         m0 = []
         m1 = []
         for t in range(PACK - 1):
-            scatter(pv[t % 2], idx4, 0, J, b_sb[:, t, :])
+            scatter(pv[t % 2], idx4, 0, J, b_sb[t // 2][:, t % 2, :])
             add_boards(t, 0, POOLS)
-            pool_board(t, 0, POOLS)
-        m0.append(tile([P, PAGE], F32, "m0_0", tag="xo_raw"))
-        m1.append(tile([P, PAGE], F32, "m1_0", tag="w2_raw"))
+        m0.append(tile([P, PAGE], F32, "m0_0", tag="xt_plane"))
+        m1.append(tile([P, PAGE], F32, "m1_0", tag="xt_raw"))
         m0.append(tile([P, PAGE], F32, "m0_1", tag="pw0"))
         m1.append(tile([P, PAGE], F32, "m1_1", tag="pw1"))
         for window in m0 + m1:
-            zero(nc.gpsimd, window[:])
+            zero(nc.vector, window[:])
 
         last = PACK - 1
-        scatter(pv[last % 2], idx4, 0, J, b_sb[:, last, :])
-        p_sb = tile([P, 2, POOLS], F32, "p_sb")
-        p_first = psum.tile([P, HALF], F32, name="p_first")
-        p_next = psum.tile([P, HALF], F32, name="p_next")
-        p_late = psum.tile([P, 2, HALF], F32, name="p_late")
+        scatter(pv[last % 2], idx4, 0, J, b_sb[last // 2][:, last % 2, :])
+        p_sb = [tile([P, HALF], F32, "p_sb%d" % u) for u in range(2)]
+        p_rest = tile([P, 2, HALF], F32, "p_rest")
+        p_first = psum.tile([P, HALF], F32, name="p_first", tag="bank0")
+        p_next = psum.tile([P, HALF], F32, name="p_next", tag="bank1")
+        p_late = psum.tile([P, 2, HALF], F32, name="p_late", tag="bank2")
 
         def multiply_p(target, u, h):
             pools = slice(HALF * h, HALF * (h + 1))
@@ -263,28 +263,32 @@ def tile_picked_tokens_plain_two_pooledboard_store_divergence_kernel(
             )
 
         quarters = (0, QUARTER)
-        for step in (add_boards, pool_board):
-            for o0 in quarters:
-                step(last, o0, QUARTER)
+        hid = tile([P, HALF, PACK], BF16, "hid_first", tag="hid")
         for o0 in quarters:
-            quantise(o0, QUARTER)
+            add_boards(last, o0, QUARTER)
+        for o0 in quarters:
+            pool_boards(hid, o0, o0, QUARTER)
+        for o0 in quarters:
+            quantise(hid, o0, o0, QUARTER)
         multiply_p(p_first[:], 0, 0)
         multiply_p(p_next[:], 1, 0)
-        nc.scalar.activation(p_sb[:, 0, 0:HALF], p_first[:], COPY)
-        scatter(m0[0], idx6, 0, HALF, p_sb[:, 0, 0:HALF])
-        scatter(m1[0], idx7, 0, HALF, p_sb[:, 0, 0:HALF])
+        nc.scalar.activation(p_sb[0][:], p_first[:], COPY)
+        scatter(m0[0], idx6, 0, HALF, p_sb[0][:])
+        scatter(m1[0], idx7, 0, HALF, p_sb[0][:])
+        nc.vector.tensor_copy(p_sb[1][:], p_next[:])
+        scatter(m0[1], idx6, 0, HALF, p_sb[1][:])
+        scatter(m1[1], idx7, 0, HALF, p_sb[1][:])
 
         add_boards(last, HALF, HALF)
-        pool_board(last, HALF, HALF)
-        quantise(HALF, HALF)
+        hid = tile([P, HALF, PACK], BF16, "hid_second", tag="hid")
+        pool_boards(hid, 0, HALF, HALF)
+        quantise(hid, 0, HALF, HALF)
         for u in (0, 1):
             multiply_p(p_late[:, u, :], u, 1)
-        nc.vector.tensor_copy(p_sb[:, :, HALF:POOLS], p_late[:])
-        nc.vector.tensor_copy(p_sb[:, 1, 0:HALF], p_next[:])
-        scatter(m0[0], idx6, HALF, HALF, p_sb[:, 0, HALF:POOLS])
-        scatter(m1[0], idx7, HALF, HALF, p_sb[:, 0, HALF:POOLS])
-        scatter(m0[1], idx6, 0, J, p_sb[:, 1, :])
-        scatter(m1[1], idx7, 0, J, p_sb[:, 1, :])
+        nc.vector.tensor_copy(p_rest[:], p_late[:])
+        for u in (0, 1):
+            scatter(m0[u], idx6, HALF, HALF, p_rest[:, u, :])
+            scatter(m1[u], idx7, HALF, HALF, p_rest[:, u, :])
 
         y = tile([P, 2, PAGE], F32, "y")
         nc.vector.tensor_tensor(y[:, 0, :], m0[0][:], m1[0][:], ALU.subtract)

@@ -88,24 +88,20 @@ def tile_picked_tokens_plain_two_pooledboard_store_divergence_kernel(
         pw = [tile([P, BOARD], F32, "pw%d" % t) for t in range(PACK)]
         w2_spread = tile([P, R], U8, "w2_spread")
         xo_plane = tile([P, STORE], U8, "xo_plane")
-        for t in range(PACK - 1):
-            zero(nc.vector, pw[t][:])
-        zero(nc.gpsimd, xo_plane[:])
-        zero(nc.gpsimd, w2_spread[:])
-        zero(nc.gpsimd, pw[PACK - 1][:])
         vs_plane = tile([P, STORE], U8, "vs_plane")
-        zero(nc.gpsimd, vs_plane[:])
+        for target in [w2_spread, xo_plane, vs_plane] + pw:
+            zero(nc.vector, target[:])
 
         xo_raw = tile([P, STORE], U32, "xo_raw")
         w2_raw = tile([P, 2 * R], U8, "w2_raw")
         vs_raw = tile([P, STORE], U16, "vs_raw")
+        load_scales(w2_spread, w2_scales)
         nc.sync.dma_start(
             xo_raw[:].bitcast(I32), xo_words[0].rearrange("p n t -> p (n t)").bitcast(I32)
         )
         nc.sync.dma_start(w2_raw[:].bitcast(I32), w2_words[0].bitcast(I32))
         idx2 = load_list(offs2, "idx2")
         load_scales(xo_plane, xo_scales)
-        load_scales(w2_spread, w2_scales)
         idx4 = load_list(offs4, "idx4")
         nc.sync.dma_start(vs_raw[:].bitcast(I32), vs_words[0].bitcast(I32))
         idx5 = load_list(offs5, "idx5")
@@ -173,10 +169,10 @@ def tile_picked_tokens_plain_two_pooledboard_store_divergence_kernel(
         xo_codes = tile([P, J], U32, "xo_codes", tag="xt_codes")
         xo_bytes = tile([P, J], U8, "xo_bytes", tag="xt_bytes")
         b_sb = [tile([P, 2, J], F32, "b_sb%d" % pair) for pair in range(2)]
-        nc.gpsimd.tensor_copy(
+        nc.vector.tensor_copy(
             w2_codes[:], w2_raw[:].rearrange("p (m t e) -> p t m e", t=PACK, e=2)
         )
-        deal_scales(nc.gpsimd, w2_plane, w2_spread)
+        deal_scales(nc.vector, w2_plane, w2_spread)
         nc.vector.tensor_copy(xo_codes[:], xo_raw[:].indirect(idx2[:]))
         nc.vector.tensor_copy(xo_bytes[:], xo_plane[:].indirect(idx2[:]))
         pv = [tile([P, BOARD], F32, "pv0", tag="xo_raw"), tile([P, BOARD], F32, "pv1", tag="xo_plane")]
@@ -202,21 +198,27 @@ def tile_picked_tokens_plain_two_pooledboard_store_divergence_kernel(
         nc.vector.tensor_copy(vs_codes[:].bitcast(U16), vs_raw[:].indirect(idx5[:]))
         nc.vector.tensor_copy(vs_bytes[:], vs_plane[:].indirect(idx5[:]))
 
-        pg = tile([P, PACK, BOARD], F32, "pg", tag="vs_raw")
+        pooled = tile([P, PACK, POOLS], BF16, "pooled")
 
-        def add_boards(t, o0, count):
+        def add_boards(pg, g0, t, o0, count):
             cols = slice(2 * o0, 2 * (o0 + count))
-            nc.vector.tensor_tensor(pg[:, t, cols], pw[t][:, cols], pv[t % 2][:, cols], ALU.add)
-
-        def pool_boards(hid, h0, o0, count):
-            pairs = pg[:, :, 2 * o0 : 2 * (o0 + count)].rearrange(
-                "p t (c i e) -> p c t i e", i=RUN, e=2
-            )
             nc.vector.tensor_tensor(
+                pg[:, g0 : g0 + count, :].rearrange("p o e -> p (o e)"),
+                pw[t][:, cols],
+                pv[t % 2][:, cols],
+                ALU.add,
+            )
+
+        def pool_board(pg, g0, t, o0, count):
+            pairs = pg[:, g0 : g0 + count, :]
+            nc.vector.tensor_tensor(
+                pooled[:, t, o0 : o0 + count], pairs[:, :, 0], pairs[:, :, 1], ALU.max
+            )
+
+        def interleave(hid, h0, o0, count):
+            nc.vector.tensor_copy(
                 hid[:, h0 : h0 + count, :].rearrange("p (c i) t -> p c t i", i=RUN),
-                pairs[:, :, :, :, 0],
-                pairs[:, :, :, :, 1],
-                ALU.max,
+                pooled[:, :, o0 : o0 + count].rearrange("p t (c i) -> p c t i", i=RUN),
             )
 
         hid_codes = tile([P, POOLS], U32, "hid_codes")
@@ -232,9 +234,11 @@ def tile_picked_tokens_plain_two_pooledboard_store_divergence_kernel(
 
         m0 = []
         m1 = []
+        pg = tile([P, POOLS, 2], F32, "pg", tag="vs_raw")
         for t in range(PACK - 1):
             scatter(pv[t % 2], idx4, 0, J, b_sb[t // 2][:, t % 2, :])
-            add_boards(t, 0, POOLS)
+            add_boards(pg, 0, t, 0, POOLS)
+            pool_board(pg, 0, t, 0, POOLS)
         m0.append(tile([P, PAGE], F32, "m0_0", tag="xt_plane"))
         m1.append(tile([P, PAGE], F32, "m1_0", tag="xt_raw"))
         m0.append(tile([P, PAGE], F32, "m0_1", tag="pw0"))
@@ -263,11 +267,13 @@ def tile_picked_tokens_plain_two_pooledboard_store_divergence_kernel(
             )
 
         quarters = (0, QUARTER)
-        hid = tile([P, HALF, PACK], BF16, "hid_first", tag="hid")
+        hid = tile([P, HALF, PACK], BF16, "hid_first")
         for o0 in quarters:
-            add_boards(last, o0, QUARTER)
+            add_boards(pg, o0, last, o0, QUARTER)
         for o0 in quarters:
-            pool_boards(hid, o0, o0, QUARTER)
+            pool_board(pg, o0, last, o0, QUARTER)
+        for o0 in quarters:
+            interleave(hid, o0, o0, QUARTER)
         for o0 in quarters:
             quantise(hid, o0, o0, QUARTER)
         multiply_p(p_first[:], 0, 0)
@@ -279,9 +285,11 @@ def tile_picked_tokens_plain_two_pooledboard_store_divergence_kernel(
         scatter(m0[1], idx6, 0, HALF, p_sb[1][:])
         scatter(m1[1], idx7, 0, HALF, p_sb[1][:])
 
-        add_boards(last, HALF, HALF)
-        hid = tile([P, HALF, PACK], BF16, "hid_second", tag="hid")
-        pool_boards(hid, 0, HALF, HALF)
+        pg = tile([P, HALF, 2], F32, "pg_second", tag="hid_first")
+        hid = tile([P, HALF, PACK], BF16, "hid_second")
+        add_boards(pg, 0, last, HALF, HALF)
+        pool_board(pg, 0, last, HALF, HALF)
+        interleave(hid, 0, HALF, HALF)
         quantise(hid, 0, HALF, HALF)
         for u in (0, 1):
             multiply_p(p_late[:, u, :], u, 1)

@@ -59,8 +59,9 @@ def tile_picked_tokens_plain_two_pooledboard_store_divergence_kernel(
                     scales[0, 4 * q : 4 * q + 4, :].bitcast(I32),
                 )
 
-        def deal_scales(engine, dealt, plane):
-            engine.tensor_copy(dealt[:], plane[:].rearrange("p (m t) -> p t m", t=PACK))
+        def deal_scales(dealt, plane, t0, t1):
+            by_tile = plane[:].rearrange("p (m t) -> p t m", t=PACK)
+            nc.vector.tensor_copy(dealt[:, t0:t1, :], by_tile[:, t0:t1, :])
 
         def scatter(window, held, start, count, values):
             nc.scalar.activation(window[:].indirect(entries(held, start, count)), values, COPY)
@@ -88,8 +89,7 @@ def tile_picked_tokens_plain_two_pooledboard_store_divergence_kernel(
         pw = [tile([P, BOARD], F32, "pw%d" % t) for t in range(PACK)]
         w2_spread = tile([P, R], U8, "w2_spread")
         xo_plane = tile([P, STORE], U8, "xo_plane")
-        vs_plane = tile([P, STORE], U8, "vs_plane")
-        for target in [w2_spread, xo_plane, vs_plane] + pw:
+        for target in [w2_spread, xo_plane] + pw:
             zero(nc.vector, target[:])
 
         xo_raw = tile([P, STORE], U32, "xo_raw")
@@ -105,7 +105,6 @@ def tile_picked_tokens_plain_two_pooledboard_store_divergence_kernel(
         idx4 = load_list(offs4, "idx4")
         nc.sync.dma_start(vs_raw[:].bitcast(I32), vs_words[0].bitcast(I32))
         idx5 = load_list(offs5, "idx5")
-        load_scales(vs_plane, vs_scales)
         idx6 = load_list(offs6, "idx6")
         idx7 = load_list(offs7, "idx7")
 
@@ -137,7 +136,7 @@ def tile_picked_tokens_plain_two_pooledboard_store_divergence_kernel(
             nc.vector.tensor_copy(
                 w_spread[32 * q : 32 * q + 4, :].bitcast(I32), w_staged[:, q, :].bitcast(I32)
             )
-        deal_scales(nc.vector, w_plane, w_spread)
+        deal_scales(w_plane, w_spread, 0, 1)
         nc.vector.tensor_copy(w_codes[:, 0, :], w_by_row[:, :, 0])
         gathered = gather_xt(0)
         first = psum.tile([P, 1, HALF], F32, name="a_first", tag="bank0")
@@ -148,6 +147,7 @@ def tile_picked_tokens_plain_two_pooledboard_store_divergence_kernel(
         nc.vector.tensor_copy(
             w_codes[:, 1:PACK, :].rearrange("p t m -> p m t"), w_by_row[:, :, 1:PACK]
         )
+        deal_scales(w_plane, w_spread, 1, PACK)
 
         def put_a(h, tiles, gathered, tag):
             bank = psum.tile([P, len(tiles), HALF], F32, name="a_%d_%d" % (h, tiles[0]), tag=tag)
@@ -168,20 +168,20 @@ def tile_picked_tokens_plain_two_pooledboard_store_divergence_kernel(
         w2_plane = tile([P, PACK, P], U8, "w2_plane", tag="w_plane")
         xo_codes = tile([P, J], U32, "xo_codes", tag="xt_codes")
         xo_bytes = tile([P, J], U8, "xo_bytes", tag="xt_bytes")
-        b_sb = [tile([P, 2, J], F32, "b_sb%d" % pair) for pair in range(2)]
         nc.vector.tensor_copy(
             w2_codes[:], w2_raw[:].rearrange("p (m t e) -> p t m e", t=PACK, e=2)
         )
-        deal_scales(nc.vector, w2_plane, w2_spread)
+        deal_scales(w2_plane, w2_spread, 0, PACK)
         nc.vector.tensor_copy(xo_codes[:], xo_raw[:].indirect(idx2[:]))
         nc.vector.tensor_copy(xo_bytes[:], xo_plane[:].indirect(idx2[:]))
         pv = [tile([P, BOARD], F32, "pv0", tag="xo_raw"), tile([P, BOARD], F32, "pv1", tag="xo_plane")]
         for window in pv:
             zero(nc.vector, window[:])
-        for pair in range(2):
-            bank = psum.tile([P, 2, J], F32, name="b_bank%d" % pair)
-            for u in range(2):
-                t = 2 * pair + u
+        b_sb = []
+        for tiles in ([0], [1], [2, 3]):
+            bank = psum.tile([P, len(tiles), J], F32, name="b_bank%d" % tiles[0])
+            values = tile([P, len(tiles), J], F32, "b_sb%d" % tiles[0])
+            for u, t in enumerate(tiles):
                 nc.tensor.matmul_mx(
                     out=bank[:, u, :],
                     lhsT=w2_codes[:, t, :, :].rearrange("p m e -> p (m e)").bitcast(FP4X4),
@@ -191,63 +191,63 @@ def tile_picked_tokens_plain_two_pooledboard_store_divergence_kernel(
                     start=True,
                     stop=True,
                 )
-            nc.vector.tensor_copy(b_sb[pair][:], bank[:])
+                b_sb.append(values[:, u, :])
+            nc.vector.tensor_copy(values[:], bank[:])
 
+        vs_plane = tile([P, STORE], U8, "vs_plane", tag="xt_plane")
+        zero(nc.vector, vs_plane[:])
+        load_scales(vs_plane, vs_scales)
         vs_codes = tile([P, 2 * J], U8, "vs_codes", tag="w_codes")
         vs_bytes = tile([P, J], U8, "vs_bytes", tag="w_plane")
         nc.vector.tensor_copy(vs_codes[:].bitcast(U16), vs_raw[:].indirect(idx5[:]))
         nc.vector.tensor_copy(vs_bytes[:], vs_plane[:].indirect(idx5[:]))
 
-        pooled = tile([P, PACK, POOLS], BF16, "pooled")
+        pieces = [(0, QUARTER), (QUARTER, QUARTER), (HALF, HALF)]
+        pooled = [tile([P, PACK, count], BF16, "pooled%d" % o0) for o0, count in pieces]
 
-        def add_boards(pg, g0, t, o0, count):
+        def add_boards(pg, t, o0, count):
             cols = slice(2 * o0, 2 * (o0 + count))
             nc.vector.tensor_tensor(
-                pg[:, g0 : g0 + count, :].rearrange("p o e -> p (o e)"),
-                pw[t][:, cols],
-                pv[t % 2][:, cols],
-                ALU.add,
+                pg.rearrange("p o e -> p (o e)"), pw[t][:, cols], pv[t % 2][:, cols], ALU.add
             )
 
-        def pool_board(pg, g0, t, o0, count):
-            pairs = pg[:, g0 : g0 + count, :]
-            nc.vector.tensor_tensor(
-                pooled[:, t, o0 : o0 + count], pairs[:, :, 0], pairs[:, :, 1], ALU.max
-            )
+        def pool_board(target, pg):
+            nc.vector.tensor_tensor(target, pg[:, :, 0], pg[:, :, 1], ALU.max)
 
-        def interleave(hid, h0, o0, count):
+        def interleave(hid, planes):
             nc.vector.tensor_copy(
-                hid[:, h0 : h0 + count, :].rearrange("p (c i) t -> p c t i", i=RUN),
-                pooled[:, :, o0 : o0 + count].rearrange("p t (c i) -> p c t i", i=RUN),
+                hid[:].rearrange("p (c i) t -> p c t i", i=RUN),
+                planes[:].rearrange("p t (c i) -> p c t i", i=RUN),
             )
 
         hid_codes = tile([P, POOLS], U32, "hid_codes")
         hid_bytes = tile([P, POOLS], U8, "hid_bytes")
 
-        def quantise(hid, h0, o0, count):
+        def quantise(hid, o0, count):
             pools = slice(o0, o0 + count)
             nc.vector.quantize_mx(
                 out=hid_codes[:, pools].bitcast(FP8X4),
                 scales=hid_bytes[:, pools],
-                in_=hid[:, h0 : h0 + count, :].rearrange("p o t -> p (o t)"),
+                in_=hid[:].rearrange("p o t -> p (o t)"),
             )
 
         m0 = []
         m1 = []
         pg = tile([P, POOLS, 2], F32, "pg", tag="vs_raw")
         for t in range(PACK - 1):
-            scatter(pv[t % 2], idx4, 0, J, b_sb[t // 2][:, t % 2, :])
-            add_boards(pg, 0, t, 0, POOLS)
-            pool_board(pg, 0, t, 0, POOLS)
-        m0.append(tile([P, PAGE], F32, "m0_0", tag="xt_plane"))
-        m1.append(tile([P, PAGE], F32, "m1_0", tag="xt_raw"))
+            scatter(pv[t % 2], idx4, 0, J, b_sb[t])
+            add_boards(pg[:], t, 0, POOLS)
+            for planes, (o0, count) in zip(pooled, pieces):
+                pool_board(planes[:, t, :], pg[:, o0 : o0 + count, :])
+        m0.append(tile([P, PAGE], F32, "m0_0", tag="xt_codes"))
+        m1.append(tile([P, PAGE], F32, "m1_0", tag="xt_bytes"))
         m0.append(tile([P, PAGE], F32, "m0_1", tag="pw0"))
         m1.append(tile([P, PAGE], F32, "m1_1", tag="pw1"))
         for window in m0 + m1:
             zero(nc.vector, window[:])
 
         last = PACK - 1
-        scatter(pv[last % 2], idx4, 0, J, b_sb[last // 2][:, last % 2, :])
+        scatter(pv[last % 2], idx4, 0, J, b_sb[last])
         p_sb = [tile([P, HALF], F32, "p_sb%d" % u) for u in range(2)]
         p_rest = tile([P, 2, HALF], F32, "p_rest")
         p_first = psum.tile([P, HALF], F32, name="p_first", tag="bank0")
@@ -266,16 +266,16 @@ def tile_picked_tokens_plain_two_pooledboard_store_divergence_kernel(
                 stop=True,
             )
 
-        quarters = (0, QUARTER)
-        hid = tile([P, HALF, PACK], BF16, "hid_first")
-        for o0 in quarters:
-            add_boards(pg, o0, last, o0, QUARTER)
-        for o0 in quarters:
-            pool_board(pg, o0, last, o0, QUARTER)
-        for o0 in quarters:
-            interleave(hid, o0, o0, QUARTER)
-        for o0 in quarters:
-            quantise(hid, o0, o0, QUARTER)
+        sums = [tile([P, QUARTER, 2], F32, "sums%d" % n) for n in range(2)]
+        hids = [tile([P, QUARTER, PACK], BF16, "hid%d" % n) for n in range(2)]
+        for n in range(2):
+            add_boards(sums[n][:], last, *pieces[n])
+        for n in range(2):
+            pool_board(pooled[n][:, last, :], sums[n][:])
+        for n in range(2):
+            interleave(hids[n], pooled[n])
+        for n in range(2):
+            quantise(hids[n], *pieces[n])
         multiply_p(p_first[:], 0, 0)
         multiply_p(p_next[:], 1, 0)
         nc.scalar.activation(p_sb[0][:], p_first[:], COPY)
@@ -285,12 +285,12 @@ def tile_picked_tokens_plain_two_pooledboard_store_divergence_kernel(
         scatter(m0[1], idx6, 0, HALF, p_sb[1][:])
         scatter(m1[1], idx7, 0, HALF, p_sb[1][:])
 
-        pg = tile([P, HALF, 2], F32, "pg_second", tag="hid_first")
-        hid = tile([P, HALF, PACK], BF16, "hid_second")
-        add_boards(pg, 0, last, HALF, HALF)
-        pool_board(pg, 0, last, HALF, HALF)
-        interleave(hid, 0, HALF, HALF)
-        quantise(hid, 0, HALF, HALF)
+        sums_rest = tile([P, HALF, 2], F32, "sums_rest", tag="hid1")
+        hid_rest = tile([P, HALF, PACK], BF16, "hid_rest")
+        add_boards(sums_rest[:], last, *pieces[2])
+        pool_board(pooled[2][:, last, :], sums_rest[:])
+        interleave(hid_rest, pooled[2])
+        quantise(hid_rest, *pieces[2])
         for u in (0, 1):
             multiply_p(p_late[:, u, :], u, 1)
         nc.vector.tensor_copy(p_rest[:], p_late[:])
@@ -298,10 +298,13 @@ def tile_picked_tokens_plain_two_pooledboard_store_divergence_kernel(
             scatter(m0[u], idx6, HALF, HALF, p_rest[:, u, :])
             scatter(m1[u], idx7, HALF, HALF, p_rest[:, u, :])
 
-        y = tile([P, 2, PAGE], F32, "y")
-        nc.vector.tensor_tensor(y[:, 0, :], m0[0][:], m1[0][:], ALU.subtract)
-        nc.sync.dma_start(out[0:P, :], y[:, 0, :])
-        for h, queue in enumerate((nc.sync, nc.scalar)):
-            cols = slice(h * PAGE // 2, (h + 1) * PAGE // 2)
-            nc.vector.tensor_tensor(y[:, 1, cols], m0[1][:, cols], m1[1][:, cols], ALU.subtract)
-            queue.dma_start(out[P : 2 * P, cols], y[:, 1, cols])
+        stores = [
+            (0, 0, PAGE, nc.sync),
+            (1, 0, PAGE // 2, nc.sync),
+            (1, PAGE // 2, PAGE // 2, nc.scalar),
+        ]
+        for u, u0, count, queue in stores:
+            cols = slice(u0, u0 + count)
+            y = tile([P, count], F32, "y_%d_%d" % (u, u0))
+            nc.vector.tensor_tensor(y[:], m0[u][:, cols], m1[u][:, cols], ALU.subtract)
+            queue.dma_start(out[P * u : P * (u + 1), cols], y[:])

from contextlib import ExitStack

import concourse.mybir as mybir

F32 = mybir.dt.float32
BF16 = mybir.dt.bfloat16
I32 = mybir.dt.int32
U32 = mybir.dt.uint32
U16 = mybir.dt.uint16
U8 = mybir.dt.uint8
FP8X4 = mybir.dt.float8_e4m3fn_x4
FP4X4 = mybir.dt.float4_e2m1fn_x4
COPY = mybir.ActivationFunctionType.Copy
ALU = mybir.AluOpType

P = 128
PACK = 4
J = 256
R = 512
STORE = 1024
BOARD = 512
POOLS = 256
PAGE = 512
HALF = 128
QUARTER = 64
RUN = 4
FLOPS = 2 * 512 * 512 * 256 * 2 + 2 * 512 * 256 * 256


def tile_picked_tokens_plain_two_pooledboard_store_divergence_kernel(
    tc, xt_words, xt_scales, w_words, w_scales, xo_words, xo_scales, w2_words, w2_scales,
    vs_words, vs_scales, offs, offs2, offs3, offs4, offs5, offs6, offs7, out,
):
    nc = tc.nc

    with ExitStack() as ctx:
        lists = ctx.enter_context(tc.tile_pool(name="lists", bufs=1))
        sb = ctx.enter_context(tc.tile_pool(name="sb", bufs=1))
        psum = ctx.enter_context(tc.psum_pool(name="psum", bufs=1))

        def tile(shape, dtype, name, tag=None):
            return sb.tile(shape, dtype, name=name, tag=tag or name, align_bytes=64)

        def load_list(source, name):
            held = lists.tile([P, J // 16], U16, name=name)
            nc.sync.dma_start(held[:], source)
            return held

        def entries(held, start, count):
            return held[:, start // 16 : (start + count) // 16]

        def zero(engine, target):
            engine.memset(target.bitcast(I32), 0)

        def load_scales(plane, scales):
            for q in range(4):
                nc.sync.dma_start(
                    plane[32 * q : 32 * q + 4, :].bitcast(I32),
                    scales[0, 4 * q : 4 * q + 4, :].bitcast(I32),
                )

        def deal_scales(dealt, plane, t0, t1):
            by_tile = plane[:].rearrange("p (m t) -> p t m", t=PACK)
            nc.vector.tensor_copy(dealt[:, t0:t1, :], by_tile[:, t0:t1, :])

        def scatter(window, held, start, count, values):
            nc.scalar.activation(window[:].indirect(entries(held, start, count)), values, COPY)

        xt_plane = tile([P, STORE], U8, "xt_plane")
        w_spread = tile([P, R], U8, "w_spread")
        zero(nc.vector, xt_plane[:])
        zero(nc.vector, w_spread[:])

        w_staged = tile([4, 4, R], U8, "w_staged")
        xt_raw = tile([P, STORE], U16, "xt_raw")
        w_raw = tile([P, R], U32, "w_raw")
        nc.sync.dma_start(
            w_staged[:].bitcast(I32),
            w_scales[0].rearrange("(q i) n -> i q n", i=4).bitcast(I32),
        )
        nc.sync.dma_start(xt_raw[:].bitcast(I32), xt_words[0].bitcast(I32))
        nc.sync.dma_start(
            w_raw[:].bitcast(I32), w_words[0].rearrange("p n t -> p (n t)").bitcast(I32)
        )
        idx = load_list(offs, "idx")
        load_scales(xt_plane, xt_scales)
        idx3 = load_list(offs3, "idx3")

        pw = [tile([P, BOARD], F32, "pw%d" % t) for t in range(PACK)]
        w2_spread = tile([P, R], U8, "w2_spread")
        xo_plane = tile([P, STORE], U8, "xo_plane")
        for target in [w2_spread, xo_plane] + pw:
            zero(nc.vector, target[:])

        xo_raw = tile([P, STORE], U32, "xo_raw")
        w2_raw = tile([P, 2 * R], U8, "w2_raw")
        vs_raw = tile([P, STORE], U16, "vs_raw")
        load_scales(w2_spread, w2_scales)
        nc.sync.dma_start(
            xo_raw[:].bitcast(I32), xo_words[0].rearrange("p n t -> p (n t)").bitcast(I32)
        )
        nc.sync.dma_start(w2_raw[:].bitcast(I32), w2_words[0].bitcast(I32))
        idx2 = load_list(offs2, "idx2")
        load_scales(xo_plane, xo_scales)
        idx4 = load_list(offs4, "idx4")
        nc.sync.dma_start(vs_raw[:].bitcast(I32), vs_words[0].bitcast(I32))
        idx5 = load_list(offs5, "idx5")
        idx6 = load_list(offs6, "idx6")
        idx7 = load_list(offs7, "idx7")

        w_codes = tile([P, PACK, P], U32, "w_codes")
        w_plane = tile([P, PACK, P], U8, "w_plane")

        def gather_xt(h):
            codes = tile([P, 2 * HALF], U8, "xt_codes%d" % h, tag="xt_codes")
            scale_bytes = tile([P, HALF], U8, "xt_bytes%d" % h, tag="xt_bytes")
            listed = entries(idx, HALF * h, HALF)
            nc.vector.tensor_copy(codes[:].bitcast(U16), xt_raw[:].indirect(listed))
            nc.vector.tensor_copy(scale_bytes[:], xt_plane[:].indirect(listed))
            return codes, scale_bytes

        def multiply_a(target, t, gathered):
            codes, scale_bytes = gathered
            nc.tensor.matmul_mx(
                out=target,
                lhsT=w_codes[:, t, :].bitcast(FP8X4),
                lhsT_scale=w_plane[:, t, :],
                rhs=codes[:].bitcast(FP4X4),
                rhs_scale=scale_bytes[:],
                start=True,
                stop=True,
            )

        w_by_row = w_raw[:].rearrange("p (m t) -> p m t", t=PACK)
        for q in range(4):
            nc.vector.tensor_copy(
                w_spread[32 * q : 32 * q + 4, :].bitcast(I32), w_staged[:, q, :].bitcast(I32)
            )
        deal_scales(w_plane, w_spread, 0, 1)
        nc.vector.tensor_copy(w_codes[:, 0, :], w_by_row[:, :, 0])
        gathered = gather_xt(0)
        first = psum.tile([P, 1, HALF], F32, name="a_first", tag="bank0")
        multiply_a(first[:, 0, :], 0, gathered)
        a_first = tile([P, HALF], F32, "a_first_sb")
        nc.scalar.activation(a_first[:], first[:, 0, :], COPY)
        scatter(pw[0], idx3, 0, HALF, a_first[:])
        nc.vector.tensor_copy(
            w_codes[:, 1:PACK, :].rearrange("p t m -> p m t"), w_by_row[:, :, 1:PACK]
        )
        deal_scales(w_plane, w_spread, 1, PACK)

        def put_a(h, tiles, gathered, tag):
            bank = psum.tile([P, len(tiles), HALF], F32, name="a_%d_%d" % (h, tiles[0]), tag=tag)
            for u, t in enumerate(tiles):
                multiply_a(bank[:, u, :], t, gathered)
            values = tile([P, len(tiles), HALF], F32, "a_sb_%d_%d" % (h, tiles[0]))
            nc.vector.tensor_copy(values[:], bank[:])
            for u, t in enumerate(tiles):
                scatter(pw[t], idx3, HALF * h, HALF, values[:, u, :])

        put_a(0, [1], gathered, "bank1")
        put_a(0, [2, 3], gathered, "bank2")
        gathered = gather_xt(1)
        put_a(1, [0, 1], gathered, "bank3")
        put_a(1, [2, 3], gathered, "bank4")

        w2_codes = tile([P, PACK, P, 2], U8, "w2_codes", tag="w_codes")
        w2_plane = tile([P, PACK, P], U8, "w2_plane", tag="w_plane")
        xo_codes = tile([P, J], U32, "xo_codes", tag="xt_codes")
        xo_bytes = tile([P, J], U8, "xo_bytes", tag="xt_bytes")
        nc.vector.tensor_copy(
            w2_codes[:], w2_raw[:].rearrange("p (m t e) -> p t m e", t=PACK, e=2)
        )
        deal_scales(w2_plane, w2_spread, 0, PACK)
        nc.vector.tensor_copy(xo_codes[:], xo_raw[:].indirect(idx2[:]))
        nc.vector.tensor_copy(xo_bytes[:], xo_plane[:].indirect(idx2[:]))
        pv = [tile([P, BOARD], F32, "pv0", tag="xo_raw"), tile([P, BOARD], F32, "pv1", tag="xo_plane")]
        for window in pv:
            zero(nc.vector, window[:])
        b_sb = []
        for tiles in ([0], [1], [2, 3]):
            bank = psum.tile([P, len(tiles), J], F32, name="b_bank%d" % tiles[0])
            values = tile([P, len(tiles), J], F32, "b_sb%d" % tiles[0])
            for u, t in enumerate(tiles):
                nc.tensor.matmul_mx(
                    out=bank[:, u, :],
                    lhsT=w2_codes[:, t, :, :].rearrange("p m e -> p (m e)").bitcast(FP4X4),
                    lhsT_scale=w2_plane[:, t, :],
                    rhs=xo_codes[:].bitcast(FP8X4),
                    rhs_scale=xo_bytes[:],
                    start=True,
                    stop=True,
                )
                b_sb.append(values[:, u, :])
            nc.vector.tensor_copy(values[:], bank[:])

        vs_plane = tile([P, STORE], U8, "vs_plane", tag="xt_plane")
        zero(nc.vector, vs_plane[:])
        load_scales(vs_plane, vs_scales)
        vs_codes = tile([P, 2 * J], U8, "vs_codes", tag="w_codes")
        vs_bytes = tile([P, J], U8, "vs_bytes", tag="w_plane")
        nc.vector.tensor_copy(vs_codes[:].bitcast(U16), vs_raw[:].indirect(idx5[:]))
        nc.vector.tensor_copy(vs_bytes[:], vs_plane[:].indirect(idx5[:]))

        pieces = [(0, QUARTER), (QUARTER, QUARTER), (HALF, HALF)]
        pooled = [tile([P, PACK, count], BF16, "pooled%d" % o0) for o0, count in pieces]

        def add_boards(pg, t, o0, count):
            cols = slice(2 * o0, 2 * (o0 + count))
            nc.vector.tensor_tensor(
                pg.rearrange("p o e -> p (o e)"), pw[t][:, cols], pv[t % 2][:, cols], ALU.add
            )

        def pool_board(target, pg):
            nc.vector.tensor_tensor(target, pg[:, :, 0], pg[:, :, 1], ALU.max)

        def interleave(hid, planes):
            nc.vector.tensor_copy(
                hid[:].rearrange("p (c i) t -> p c t i", i=RUN),
                planes[:].rearrange("p t (c i) -> p c t i", i=RUN),
            )

        hid_codes = tile([P, POOLS], U32, "hid_codes")
        hid_bytes = tile([P, POOLS], U8, "hid_bytes")

        def quantise(hid, o0, count):
            pools = slice(o0, o0 + count)
            nc.vector.quantize_mx(
                out=hid_codes[:, pools].bitcast(FP8X4),
                scales=hid_bytes[:, pools],
                in_=hid[:].rearrange("p o t -> p (o t)"),
            )

        m0 = []
        m1 = []
        pg = tile([P, POOLS, 2], F32, "pg", tag="vs_raw")
        for t in range(PACK - 1):
            scatter(pv[t % 2], idx4, 0, J, b_sb[t])
            add_boards(pg[:], t, 0, POOLS)
            for planes, (o0, count) in zip(pooled, pieces):
                pool_board(planes[:, t, :], pg[:, o0 : o0 + count, :])
        m0.append(tile([P, PAGE], F32, "m0_0", tag="xt_codes"))
        m1.append(tile([P, PAGE], F32, "m1_0", tag="xt_bytes"))
        m0.append(tile([P, PAGE], F32, "m0_1", tag="pw0"))
        m1.append(tile([P, PAGE], F32, "m1_1", tag="pw1"))
        for window in m0 + m1:
            zero(nc.vector, window[:])

        last = PACK - 1
        scatter(pv[last % 2], idx4, 0, J, b_sb[last])
        p_sb = [tile([P, HALF], F32, "p_sb%d" % u) for u in range(2)]
        p_rest = tile([P, 2, HALF], F32, "p_rest")
        p_first = psum.tile([P, HALF], F32, name="p_first", tag="bank0")
        p_next = psum.tile([P, HALF], F32, name="p_next", tag="bank1")
        p_late = psum.tile([P, 2, HALF], F32, name="p_late", tag="bank2")

        def multiply_p(target, u, h):
            pools = slice(HALF * h, HALF * (h + 1))
            nc.tensor.matmul_mx(
                out=target,
                lhsT=vs_codes[:, 2 * P * u : 2 * P * (u + 1)].bitcast(FP4X4),
                lhsT_scale=vs_bytes[:, P * u : P * (u + 1)],
                rhs=hid_codes[:, pools].bitcast(FP8X4),
                rhs_scale=hid_bytes[:, pools],
                start=True,
                stop=True,
            )

        sums = [tile([P, QUARTER, 2], F32, "sums%d" % n) for n in range(2)]
        hids = [tile([P, QUARTER, PACK], BF16, "hid%d" % n) for n in range(2)]
        for n in range(2):
            add_boards(sums[n][:], last, *pieces[n])
        for n in range(2):
            pool_board(pooled[n][:, last, :], sums[n][:])
        for n in range(2):
            interleave(hids[n], pooled[n])
        for n in range(2):
            quantise(hids[n], *pieces[n])
        multiply_p(p_first[:], 0, 0)
        multiply_p(p_next[:], 1, 0)
        nc.scalar.activation(p_sb[0][:], p_first[:], COPY)
        scatter(m0[0], idx6, 0, HALF, p_sb[0][:])
        scatter(m1[0], idx7, 0, HALF, p_sb[0][:])
        nc.vector.tensor_copy(p_sb[1][:], p_next[:])
        scatter(m0[1], idx6, 0, HALF, p_sb[1][:])
        scatter(m1[1], idx7, 0, HALF, p_sb[1][:])

        sums_rest = tile([P, HALF, 2], F32, "sums_rest", tag="hid1")
        hid_rest = tile([P, HALF, PACK], BF16, "hid_rest")
        add_boards(sums_rest[:], last, *pieces[2])
        pool_board(pooled[2][:, last, :], sums_rest[:])
        interleave(hid_rest, pooled[2])
        quantise(hid_rest, *pieces[2])
        for u in (0, 1):
            multiply_p(p_late[:, u, :], u, 1)
        nc.vector.tensor_copy(p_rest[:], p_late[:])
        for u in (0, 1):
            scatter(m0[u], idx6, HALF, HALF, p_rest[:, u, :])
            scatter(m1[u], idx7, HALF, HALF, p_rest[:, u, :])

        stores = [
            (0, 0, PAGE, nc.sync),
            (1, 0, PAGE // 2, nc.sync),
            (1, PAGE // 2, PAGE // 2, nc.scalar),
        ]
        for u, u0, count, queue in stores:
            cols = slice(u0, u0 + count)
            y = tile([P, count], F32, "y_%d_%d" % (u, u0))
            nc.vector.tensor_tensor(y[:], m0[u][:, cols], m1[u][:, cols], ALU.subtract)
            queue.dma_start(out[P * u : P * (u + 1), cols], y[:])
